import numpy as np
import ml_dtypes


def mxq(x, axis, fmt="e4m3"):
    dtype, down = {"e4m3": (ml_dtypes.float8_e4m3fn, 7), "e5m2": (ml_dtypes.float8_e5m2, 14)}[fmt]
    v = np.moveaxis(np.asarray(x, np.float32).astype(ml_dtypes.bfloat16).astype(np.float64), axis, -1)
    blocks = v.reshape(v.shape[:-1] + (-1, 32))
    amax = np.abs(blocks).max(-1, keepdims=True)
    byte = np.maximum(np.where(amax > 0, np.frexp(amax)[1] - 1 + 127, 0) - down, 1)
    scale = np.exp2(byte - 127.0)
    codes = (blocks / scale).astype(np.float32).astype(dtype).astype(np.float64)
    return np.moveaxis((codes * scale).reshape(v.shape), -1, axis)


WIDE = False


def mx_kscale(k):
    if not WIDE:
        return np.ones(k)
    levels = np.array([10, -10, 5, -5, 0])
    if k % 512:
        return np.exp2(np.random.permutation(np.resize(levels, k // 32))).repeat(32)
    a = np.empty((k // 512, 16))
    for p in range(k // 512):
        a[p, :8] = np.random.permutation(np.resize(levels, 8))
        for g in range(8):
            far = levels[np.abs(levels - a[p, g]) >= 10]
            a[p, g + 8] = far[np.random.randint(len(far))]
    return np.exp2(a.ravel()).repeat(32)


BF16 = ml_dtypes.bfloat16


def bf(x):
    return np.asarray(x, np.float32).astype(BF16)


def f64(x):
    return np.asarray(x).astype(np.float64)


E2M1 = np.array([0.0, 0.5, 1.0, 1.5, 2.0, 3.0, 4.0, 6.0, -0.0, -0.5, -1.0, -1.5, -2.0, -3.0, -4.0, -6.0])


def pack_weight(w, fmt):
    k, n = w.shape
    w = f64(bf(w)).reshape(k // 32, 32, n)
    amax = np.abs(w).max(1)
    if fmt == "e4m3":
        byte = np.frexp(amax)[1] - 1 + 127 - 7
    else:
        mant, ex = np.frexp(amax / 6.0)
        byte = np.where(mant > 0.5, ex, ex - 1) + 127
    byte = np.clip(np.where(amax > 0, byte, 1), 1, 254)
    scaled = (w * np.exp2(127.0 - byte)[:, None, :]).reshape(k, n).astype(np.float32)
    by_word = np.ascontiguousarray(scaled.reshape(k // 512, 128, 4, n).transpose(0, 1, 3, 2))
    if fmt == "e4m3":
        words = by_word.astype(ml_dtypes.float8_e4m3fn).view(np.uint8)
    else:
        c = by_word.astype(ml_dtypes.float4_e2m1fn).view(np.uint8) & 0xF
        words = c[..., 0::2] | (c[..., 1::2] << 4)
    return np.ascontiguousarray(words), np.ascontiguousarray(byte.astype(np.uint8).reshape(k // 512, 16, n))


def unpack_weight(words, scales, fmt):
    g, p, n, _ = words.shape
    if fmt == "e4m3":
        vals = np.ascontiguousarray(words).view(ml_dtypes.float8_e4m3fn).astype(np.float64)
    else:
        nib = np.empty((g, p, n, 4), np.uint8)
        nib[..., 0::2] = words & 0xF
        nib[..., 1::2] = words >> 4
        vals = E2M1[nib]
    vals = vals * np.repeat(np.exp2(scales.astype(np.float64) - 127.0), 8, axis=1)[..., None]
    return vals.transpose(0, 1, 3, 2).reshape(g * 512, n)
def pack4(w):
    words, scales = pack_weight(w, "e2m1")
    return words.reshape(words.shape[0], 128, -1), scales


def unpack4(words, scales):
    return unpack_weight(words.reshape(words.shape[0], 128, -1, 2), scales, "e2m1")


V, D, P, L, C = 2048, 1536, 1024, 512, 512


def setup_inputs():
    m, s, t = mx_kscale(P), mx_kscale(L), mx_kscale(D)
    vox_words, vox_scales = pack4(np.random.standard_normal((P, V)) / np.sqrt(P) * m[:, None])
    chan_words, chan_scales = pack4(np.random.standard_normal((P, D)) / D ** 0.25 / m[:, None] * t)
    return {"vox_words": vox_words, "vox_scales": vox_scales,
            "chan_words": chan_words, "chan_scales": chan_scales,
            "ratio": bf(np.exp(0.7 * np.random.standard_normal((D, L)))),
            "bin_weight": bf((1 + 0.1 * np.random.standard_normal(L)) * s),
            "unmix": bf(np.random.standard_normal((L, C)) / np.sqrt(L) / s[:, None]),
            "coupling": bf(np.random.uniform(0.5, 1.5, D) / t)}


def reference(vox_words, vox_scales, chan_words, chan_scales, ratio, bin_weight, unmix, coupling):
    inv = unpack4(vox_words, vox_scales).T @ unpack4(chan_words, chan_scales)
    od = np.log(f64(ratio)) * f64(bin_weight)
    hb = mxq(od, 1, "e4m3") @ mxq(f64(unmix), 0, "e4m3")
    hb = hb * f64(coupling)[:, None]
    return mxq(inv, 1, "e4m3") @ mxq(hb, 0, "e4m3")

@@ -1,0 +1,311 @@
+from contextlib import ExitStack
+
+import concourse.mybir as mybir
+from concourse.masks import make_identity
+
+V, D, MODES, L, C = 2048, 1536, 1024, 512, 512
+FLOPS = 2 * V * D * MODES + 2 * D * L * C + 2 * V * D * C
+
+F32 = mybir.dt.float32
+BF16 = mybir.dt.bfloat16
+I32 = mybir.dt.int32
+U32 = mybir.dt.uint32
+U8 = mybir.dt.uint8
+FP8X4 = mybir.dt.float8_e4m3fn_x4
+FP4X4 = mybir.dt.float4_e2m1fn_x4
+ACT = mybir.ActivationFunctionType
+ALU = mybir.AluOpType
+
+P = 128
+PACK = 4
+K_PASS = P * PACK
+MODE_PASSES = MODES // K_PASS
+GROUPS = D // K_PASS
+SLICES = V // K_PASS
+ALIGN = 64
+
+TURN_AT = (2, 11, 21)
+WEIGH_AT = (5, 14, 24)
+HB_AT = (12, 22, 32)
+OUT_FROM = 37
+VECTOR_STEPS = (0, 1, 2, 3, 12, 22)
+WIDE_FROM = 48
+HELD_BACK = 6
+
+
+def tile_optical_tomography_unmixing_s12_kernel(
+    tc, vox_words, vox_scales, chan_words, chan_scales, ratio, bin_weight, unmix, coupling, out
+):
+    nc = tc.nc
+    with ExitStack() as ctx:
+        keep = ctx.enter_context(tc.tile_pool(name="keep", bufs=1))
+        stage = ctx.enter_context(tc.tile_pool(name="stage", bufs=2))
+        stream = ctx.enter_context(tc.tile_pool(name="stream", bufs=4))
+        psum = ctx.enter_context(tc.psum_pool(name="psum", bufs=8))
+        ctx.enter_context(tc.manual_schedule())
+
+        def kept(name, shape, dtype):
+            return keep.tile(shape, dtype, name=name, align_bytes=ALIGN)
+
+        def new_bank(dtype):
+            width = K_PASS if dtype == F32 else 2 * K_PASS
+            return psum.tile([P, width], dtype, name="bank", tag="bank")
+
+        vox_codes = [kept("vox_codes%d" % s, [P, MODE_PASSES, 2 * K_PASS], U8) for s in range(SLICES)]
+        vox_plane_first = kept("vox_plane_first", [P, MODE_PASSES, K_PASS], U8)
+        vox_plane_rest = kept("vox_plane_rest", [P, MODE_PASSES, V - K_PASS], U8)
+        chan_raw = [kept("chan_raw%d" % g, [P, MODE_PASSES, 2 * K_PASS], U8) for g in range(GROUPS)]
+        chan_plane_first = kept("chan_plane_first", [P, MODE_PASSES, K_PASS], U8)
+        chan_plane_rest = kept("chan_plane_rest", [P, MODE_PASSES, D - K_PASS], U8)
+        chan_codes = [kept("chan_codes%d" % g, [P, MODE_PASSES, PACK, 2 * P], U8) for g in range(GROUPS)]
+        chan_plane = [kept("chan_plane%d" % g, [P, MODE_PASSES, PACK, P], U8) for g in range(GROUPS)]
+        ratio_rows = [kept("ratio_rows%d" % g, [P, PACK, L], BF16) for g in range(GROUPS)]
+        unmix_raw = kept("unmix_raw", [P, PACK, C], BF16)
+        unmix_packed = kept("unmix_packed", [P, C, PACK], BF16)
+        unmix_codes = kept("unmix_codes", [P, C], U32)
+        unmix_plane = kept("unmix_plane", [P, C], U8)
+        weight_raw = kept("weight_raw", [P, PACK], BF16)
+        weight_run = kept("weight_run", [P, 8, PACK], F32)
+        coupling_rows = kept("coupling_rows", [P, GROUPS * P], BF16)
+        coupling_slots = kept("coupling_slots", [P, GROUPS, PACK], F32)
+        ident_f32 = kept("ident_f32", [P, P], F32)
+        ident_bf16 = kept("ident_bf16", [P, P], BF16)
+        od_codes = [kept("od_codes%d" % g, [P, K_PASS], U32) for g in range(GROUPS)]
+        od_plane = [kept("od_plane%d" % g, [P, K_PASS], U8) for g in range(GROUPS)]
+        hb_codes = [kept("hb_codes%d" % g, [P, C], U32) for g in range(GROUPS)]
+        hb_plane = [kept("hb_plane%d" % g, [P, C], U8) for g in range(GROUPS)]
+        inv_codes = {}
+        inv_plane = {}
+        for s in range(SLICES):
+            for g in range(GROUPS):
+                inv_codes[(s, g)] = kept("inv_codes%d_%d" % (s, g), [P, K_PASS], U32)
+                inv_plane[(s, g)] = kept("inv_plane%d_%d" % (s, g), [P, K_PASS], U8)
+
+        for plane in (chan_plane_first, vox_plane_first, chan_plane_rest, vox_plane_rest):
+            nc.vector.memset(plane[:].bitcast(I32), 0)
+        make_identity(nc, ident_f32[:])
+        nc.gpsimd.memset(coupling_rows[:], 0.0)
+        make_identity(nc, ident_bf16[:])
+
+        def load_codes(dst, words, index):
+            cols = slice(index * 256, (index + 1) * 256)
+            nc.sync.dma_start(out=dst[:].bitcast(I32), in_=words.bitcast(I32)[:, :, cols].rearrange("g p w -> p g w"))
+
+        def load_plane(dst, scales, cols):
+            for quad in range(4):
+                nc.sync.dma_start(
+                    out=dst[32 * quad : 32 * quad + 4, :, :].bitcast(I32),
+                    in_=scales.bitcast(I32)[:, 4 * quad : 4 * quad + 4, cols].rearrange("g r w -> r g w"),
+                )
+
+        def load_ratio(g):
+            rows = ratio[g * K_PASS : (g + 1) * K_PASS, :]
+            nc.sync.dma_start(out=ratio_rows[g][:], in_=rows.rearrange("(m j) l -> m j l", j=PACK))
+
+        first = slice(0, P)
+        load_codes(chan_raw[0], chan_words, 0)
+        load_codes(vox_codes[0], vox_words, 0)
+        load_plane(chan_plane_first, chan_scales, first)
+        load_plane(vox_plane_first, vox_scales, first)
+        load_ratio(0)
+        load_codes(chan_raw[1], chan_words, 1)
+        load_plane(chan_plane_rest, chan_scales, slice(P, D // 4))
+        nc.sync.dma_start(out=weight_raw[:], in_=bin_weight.rearrange("(p t) -> p t", t=PACK))
+        load_codes(chan_raw[2], chan_words, 2)
+        nc.sync.dma_start(out=unmix_raw[:], in_=unmix.rearrange("(p j) c -> p j c", j=PACK))
+        load_plane(vox_plane_rest, vox_scales, slice(P, V // 4))
+        load_codes(vox_codes[1], vox_words, 1)
+        nc.sync.dma_start(
+            out=coupling_rows[0:PACK, :].rearrange("t (b r) -> t b r", r=8),
+            in_=coupling.rearrange("(b t r) -> t b r", t=PACK, r=8),
+        )
+        load_ratio(1)
+        load_codes(vox_codes[2], vox_words, 2)
+        load_ratio(2)
+        load_codes(vox_codes[3], vox_words, 3)
+
+        def group_of(first_tile, rest_tile, index):
+            if index == 0:
+                return first_tile[:]
+            return rest_tile[:, :, (index - 1) * K_PASS : index * K_PASS]
+
+        def quantize(codes, plane, packed):
+            nc.vector.quantize_mx(
+                out=codes[:].bitcast(FP8X4), scales=plane[:], in_=packed[:].rearrange("p c t -> p (c t)")
+            )
+
+        def sort_channels(g):
+            nc.vector.tensor_copy(
+                out=chan_codes[g][:].bitcast(I32).rearrange("p k t (q w) -> p k t q w", w=4),
+                in_=chan_raw[g][:].bitcast(I32).rearrange("p k (q t w) -> p k t q w", t=PACK, w=4),
+            )
+            nc.vector.tensor_copy(
+                out=chan_plane[g][:].bitcast(I32).rearrange("p k t (q w) -> p k t q w", w=2),
+                in_=group_of(chan_plane_first, chan_plane_rest, g).bitcast(I32).rearrange(
+                    "p k (q t w) -> p k t q w", t=PACK, w=2
+                ),
+            )
+
+        def turn_and_log(g):
+            log_ratio = stage.tile([P, P, PACK, PACK], F32, name="log_ratio")
+            words = ratio_rows[g][:].bitcast(F32)
+            banks = []
+            for half in range(2):
+                bank = new_bank(F32)
+                for jj in range(2):
+                    for u in range(2):
+                        quarter = 2 * jj + u
+                        nc.tensor.transpose(
+                            bank[:, quarter * P : (quarter + 1) * P], words[:, 2 * half + jj, u::2], ident_f32[:]
+                        )
+                banks.append(bank)
+            for half in range(2):
+                nc.scalar.activation(
+                    out=log_ratio[:, :, 2 * half : 2 * half + 2, :].rearrange("p m j (u e) -> p m (j u) e", e=2),
+                    in_=banks[half][:].bitcast(BF16).rearrange("p (a m e) -> p m a e", a=PACK, e=2),
+                    func=ACT.Ln,
+                )
+            return log_ratio
+
+        def weigh(log_ratio):
+            od = stage.tile([P, K_PASS, PACK], BF16, name="od", align_bytes=ALIGN)
+            nc.vector.tensor_tensor(
+                out=od[:].rearrange("p (t q r) s -> p t q (r s)", t=PACK, r=8),
+                in0=log_ratio[:].rearrange("p (q t h) j s -> p t q (h j s)", t=PACK, h=2),
+                in1=weight_run[:].rearrange("p r s -> p (r s)").unsqueeze(1).unsqueeze(1).to_broadcast([P, PACK, 16, 32]),
+                op=ALU.mult,
+            )
+            return od
+
+        def spread_coupling():
+            bank = new_bank(BF16)
+            for g in range(GROUPS):
+                nc.tensor.transpose(bank[:, g * P : (g + 1) * P], coupling_rows[:, g * P : (g + 1) * P], ident_bf16[:])
+            nc.vector.tensor_copy(
+                out=coupling_slots[:], in_=bank[:, 0 : GROUPS * P].rearrange("p (g x) -> p g x", x=P)[:, :, 0:PACK]
+            )
+
+        def pack_unmix():
+            nc.vector.tensor_copy(
+                out=unmix_packed[:].rearrange("p (c i) t -> p c t i", i=4),
+                in_=unmix_raw[:].rearrange("p t (c i) -> p c t i", i=4),
+            )
+
+        def hb_block(g, hb, block):
+            cols = slice(block * P, (block + 1) * P)
+            bank = new_bank(F32)
+            for t in range(PACK):
+                slot = slice(t * P, (t + 1) * P)
+                nc.tensor.matmul_mx(
+                    out=bank[:, slot],
+                    lhsT=od_codes[g][:, slot].bitcast(FP8X4),
+                    lhsT_scale=od_plane[g][:, slot],
+                    rhs=unmix_codes[:, cols].bitcast(FP8X4),
+                    rhs_scale=unmix_plane[:, cols],
+                    start=True,
+                    stop=True,
+                )
+            nc.vector.tensor_tensor(
+                out=hb[:, cols, :],
+                in0=bank[:].rearrange("p (t c) -> p c t", t=PACK),
+                in1=coupling_slots[:, g, :].unsqueeze(1).to_broadcast([P, P, PACK]),
+                op=ALU.mult,
+            )
+
+        def inv_block(s, g, inv, block, wide, on_vector):
+            bank = new_bank(F32)
+            width = 2 * P if wide else P
+            start = (block // 2) * width if wide else block * width
+            slots = range(2 * (block % 2), 2 * (block % 2) + 2) if wide else range(PACK)
+            plane = group_of(vox_plane_first, vox_plane_rest, s)
+            for i, t in enumerate(slots):
+                for k in range(MODE_PASSES):
+                    nc.tensor.matmul_mx(
+                        out=bank[:, i * width : (i + 1) * width],
+                        lhsT=chan_codes[g][:, k, t, :].bitcast(FP4X4),
+                        lhsT_scale=chan_plane[g][:, k, t, :],
+                        rhs=vox_codes[s][:, k, 2 * start : 2 * (start + width)].bitcast(FP4X4),
+                        rhs_scale=plane[:, k, start : start + width],
+                        start=(k == 0),
+                        stop=(k == MODE_PASSES - 1),
+                    )
+            dst = inv[:, start : start + width, slots.start : slots.stop]
+            src = bank[:].rearrange("p (t v) -> p v t", v=width)
+            if on_vector:
+                nc.vector.tensor_copy(out=dst, in_=src)
+            else:
+                nc.scalar.copy(out=dst, in_=src)
+
+        def image_tile(index, on_vector):
+            s, block = divmod(index, PACK)
+            cols = slice(block * P, (block + 1) * P)
+            bank = new_bank(F32)
+            for g in range(GROUPS):
+                nc.tensor.matmul_mx(
+                    out=bank[:],
+                    lhsT=inv_codes[(s, g)][:, cols].bitcast(FP8X4),
+                    lhsT_scale=inv_plane[(s, g)][:, cols],
+                    rhs=hb_codes[g][:].bitcast(FP8X4),
+                    rhs_scale=hb_plane[g][:],
+                    start=(g == 0),
+                    stop=(g == GROUPS - 1),
+                )
+            image = stream.tile([P, C], F32, name="image")
+            if on_vector:
+                nc.vector.tensor_copy(out=image[:], in_=bank[:])
+            else:
+                nc.scalar.copy(out=image[:], in_=bank[:])
+            nc.sync.dma_start(out=out[index * P : (index + 1) * P, :], in_=image[:])
+
+        steps = SLICES * GROUPS * PACK
+        logs = {}
+        ods = {}
+        hbs = {}
+        invs = {}
+        next_image = 0
+        for step in range(steps):
+            s, rest = divmod(step, GROUPS * PACK)
+            g, block = divmod(rest, PACK)
+            if step in TURN_AT:
+                logs[TURN_AT.index(step)] = turn_and_log(TURN_AT.index(step))
+            if step == 0:
+                sort_channels(0)
+            if step == 2:
+                sort_channels(1)
+            if step == WEIGH_AT[0]:
+                nc.vector.tensor_copy(
+                    out=weight_run[:], in_=weight_raw[:].unsqueeze(1).to_broadcast([P, 8, PACK])
+                )
+            if step == 5:
+                sort_channels(2)
+            if step == 7:
+                pack_unmix()
+            if step == HB_AT[0]:
+                spread_coupling()
+            if step in WEIGH_AT:
+                ods[WEIGH_AT.index(step)] = weigh(logs[WEIGH_AT.index(step)])
+            if step == 9:
+                quantize(unmix_codes, unmix_plane, unmix_packed)
+            if step - 3 in WEIGH_AT:
+                gg = WEIGH_AT.index(step - 3)
+                quantize(od_codes[gg], od_plane[gg], ods[gg])
+            for gg in range(GROUPS):
+                if 0 <= step - HB_AT[gg] < PACK:
+                    if step == HB_AT[gg]:
+                        hbs[gg] = stage.tile([P, C, PACK], BF16, name="hb", align_bytes=ALIGN)
+                    hb_block(gg, hbs[gg], step - HB_AT[gg])
+                if step - HB_AT[gg] == PACK + 1:
+                    quantize(hb_codes[gg], hb_plane[gg], hbs[gg])
+            if block == 0:
+                invs[(s, g)] = stream.tile([P, K_PASS, PACK], BF16, name="inv", align_bytes=ALIGN)
+            inv_block(s, g, invs[(s, g)], block, step >= WIDE_FROM, step in VECTOR_STEPS)
+            if block == 1 and step > PACK:
+                done = divmod(step // PACK - 1, GROUPS)
+                quantize(inv_codes[done], inv_plane[done], invs[done])
+            if step > OUT_FROM and next_image < V // P - HELD_BACK:
+                image_tile(next_image, True)
+                next_image = next_image + 1
+        last = (SLICES - 1, GROUPS - 1)
+        quantize(inv_codes[last], inv_plane[last], invs[last])
+        for index in range(next_image, V // P):
+            image_tile(index, index % 2 == 1)

@@ -24,13 +24,17 @@ GROUPS = D // K_PASS
 SLICES = V // K_PASS
 ALIGN = 64
 
-TURN_AT = (2, 11, 21)
-WEIGH_AT = (5, 14, 24)
-HB_AT = (12, 22, 32)
-OUT_FROM = 37
-VECTOR_STEPS = (0, 1, 2, 3, 12, 22)
-WIDE_FROM = 48
-HELD_BACK = 6
+FIRST_TURN = 2
+PERIOD = 9
+WEIGH_LAG = 3
+OD_LAG = 6
+HB_LAG = 12
+HELP = 0
+WIDE_FROM = 28
+HELD_BACK = 2
+PRESORT = False
+INV_LAG = 2
+IMG_EVERY = 1
 
 
 def tile_optical_tomography_unmixing_s12_kernel(
@@ -81,19 +85,16 @@ def tile_optical_tomography_unmixing_s12_kernel(
                 inv_codes[(s, g)] = kept("inv_codes%d_%d" % (s, g), [P, K_PASS], U32)
                 inv_plane[(s, g)] = kept("inv_plane%d_%d" % (s, g), [P, K_PASS], U8)
 
-        for plane in (chan_plane_first, vox_plane_first, chan_plane_rest, vox_plane_rest):
-            nc.vector.memset(plane[:].bitcast(I32), 0)
-        make_identity(nc, ident_f32[:])
-        nc.gpsimd.memset(coupling_rows[:], 0.0)
-        make_identity(nc, ident_bf16[:])
+        nc.gpsimd.memset(chan_plane_first[:].bitcast(I32), 0)
+        nc.gpsimd.memset(vox_plane_first[:].bitcast(I32), 0)
 
         def load_codes(dst, words, index):
             cols = slice(index * 256, (index + 1) * 256)
             nc.sync.dma_start(out=dst[:].bitcast(I32), in_=words.bitcast(I32)[:, :, cols].rearrange("g p w -> p g w"))
 
-        def load_plane(dst, scales, cols):
-            for quad in range(4):
-                nc.sync.dma_start(
+        def load_plane(dst, scales, cols, queues):
+            for quad, queue in enumerate(queues):
+                queue.dma_start(
                     out=dst[32 * quad : 32 * quad + 4, :, :].bitcast(I32),
                     in_=scales.bitcast(I32)[:, 4 * quad : 4 * quad + 4, cols].rearrange("g r w -> r g w"),
                 )
@@ -103,26 +104,34 @@ def tile_optical_tomography_unmixing_s12_kernel(
             nc.sync.dma_start(out=ratio_rows[g][:], in_=rows.rearrange("(m j) l -> m j l", j=PACK))
 
         first = slice(0, P)
+        on_sync = (nc.sync, nc.sync, nc.sync, nc.sync)
         load_codes(chan_raw[0], chan_words, 0)
         load_codes(vox_codes[0], vox_words, 0)
-        load_plane(chan_plane_first, chan_scales, first)
-        load_plane(vox_plane_first, vox_scales, first)
+        load_plane(chan_plane_first, chan_scales, first, on_sync)
+        load_plane(vox_plane_first, vox_scales, first, (nc.gpsimd, nc.gpsimd, nc.sync, nc.sync))
+        make_identity(nc, ident_f32[:])
+        nc.gpsimd.memset(coupling_rows[:], 0.0)
+        make_identity(nc, ident_bf16[:])
         load_ratio(0)
         load_codes(chan_raw[1], chan_words, 1)
-        load_plane(chan_plane_rest, chan_scales, slice(P, D // 4))
-        nc.sync.dma_start(out=weight_raw[:], in_=bin_weight.rearrange("(p t) -> p t", t=PACK))
-        load_codes(chan_raw[2], chan_words, 2)
-        nc.sync.dma_start(out=unmix_raw[:], in_=unmix.rearrange("(p j) c -> p j c", j=PACK))
-        load_plane(vox_plane_rest, vox_scales, slice(P, V // 4))
-        load_codes(vox_codes[1], vox_words, 1)
-        nc.sync.dma_start(
-            out=coupling_rows[0:PACK, :].rearrange("t (b r) -> t b r", r=8),
-            in_=coupling.rearrange("(b t r) -> t b r", t=PACK, r=8),
-        )
-        load_ratio(1)
-        load_codes(vox_codes[2], vox_words, 2)
-        load_ratio(2)
-        load_codes(vox_codes[3], vox_words, 3)
+
+        def later_loads():
+            nc.vector.memset(chan_plane_rest[:].bitcast(I32), 0)
+            nc.vector.memset(vox_plane_rest[:].bitcast(I32), 0)
+            load_plane(chan_plane_rest, chan_scales, slice(P, D // 4), on_sync)
+            nc.sync.dma_start(out=weight_raw[:], in_=bin_weight.rearrange("(p t) -> p t", t=PACK))
+            load_codes(chan_raw[2], chan_words, 2)
+            nc.sync.dma_start(out=unmix_raw[:], in_=unmix.rearrange("(p j) c -> p j c", j=PACK))
+            load_plane(vox_plane_rest, vox_scales, slice(P, V // 4), on_sync)
+            load_codes(vox_codes[1], vox_words, 1)
+            nc.sync.dma_start(
+                out=coupling_rows[0:PACK, :].rearrange("t (b r) -> t b r", r=8),
+                in_=coupling.rearrange("(b t r) -> t b r", t=PACK, r=8),
+            )
+            load_ratio(1)
+            load_codes(vox_codes[2], vox_words, 2)
+            load_ratio(2)
+            load_codes(vox_codes[3], vox_words, 3)
 
         def group_of(first_tile, rest_tile, index):
             if index == 0:
@@ -146,19 +155,26 @@ def tile_optical_tomography_unmixing_s12_kernel(
                 ),
             )
 
-        def turn_and_log(g):
+        def sort_words(g):
+            words = stage.tile([P, PACK, 2, P], F32, name="words")
+            nc.vector.tensor_copy(
+                out=words[:], in_=ratio_rows[g][:].bitcast(F32).rearrange("p j (w u) -> p j u w", u=2)
+            )
+            return words
+
+        def turn_and_log(g, words):
             log_ratio = stage.tile([P, P, PACK, PACK], F32, name="log_ratio")
-            words = ratio_rows[g][:].bitcast(F32)
             banks = []
             for half in range(2):
                 bank = new_bank(F32)
                 for jj in range(2):
                     for u in range(2):
                         quarter = 2 * jj + u
-                        nc.tensor.transpose(
-                            bank[:, quarter * P : (quarter + 1) * P], words[:, 2 * half + jj, u::2], ident_f32[:]
-                        )
+                        src = words[:, 2 * half + jj, u, :] if PRESORT else ratio_rows[g][:].bitcast(F32)[:, 2 * half + jj, u::2]
+                        nc.tensor.transpose(bank[:, quarter * P : (quarter + 1) * P], src, ident_f32[:])
                 banks.append(bank)
+            if g == 1:
+                spread_coupling()
             for half in range(2):
                 nc.scalar.activation(
                     out=log_ratio[:, :, 2 * half : 2 * half + 2, :].rearrange("p m j (u e) -> p m (j u) e", e=2),
@@ -236,76 +252,89 @@ def tile_optical_tomography_unmixing_s12_kernel(
             else:
                 nc.scalar.copy(out=dst, in_=src)
 
-        def image_tile(index, on_vector):
+        def image_tile(index, cols, on_vector):
             s, block = divmod(index, PACK)
-            cols = slice(block * P, (block + 1) * P)
+            voxels = slice(block * P, (block + 1) * P)
+            width = cols.stop - cols.start
             bank = new_bank(F32)
             for g in range(GROUPS):
                 nc.tensor.matmul_mx(
-                    out=bank[:],
-                    lhsT=inv_codes[(s, g)][:, cols].bitcast(FP8X4),
-                    lhsT_scale=inv_plane[(s, g)][:, cols],
-                    rhs=hb_codes[g][:].bitcast(FP8X4),
-                    rhs_scale=hb_plane[g][:],
+                    out=bank[:, 0:width],
+                    lhsT=inv_codes[(s, g)][:, voxels].bitcast(FP8X4),
+                    lhsT_scale=inv_plane[(s, g)][:, voxels],
+                    rhs=hb_codes[g][:, cols].bitcast(FP8X4),
+                    rhs_scale=hb_plane[g][:, cols],
                     start=(g == 0),
                     stop=(g == GROUPS - 1),
                 )
-            image = stream.tile([P, C], F32, name="image")
+            image = stream.tile([P, width], F32, name="image")
             if on_vector:
-                nc.vector.tensor_copy(out=image[:], in_=bank[:])
+                nc.vector.tensor_copy(out=image[:], in_=bank[:, 0:width])
             else:
-                nc.scalar.copy(out=image[:], in_=bank[:])
-            nc.sync.dma_start(out=out[index * P : (index + 1) * P, :], in_=image[:])
+                nc.scalar.copy(out=image[:], in_=bank[:, 0:width])
+            nc.sync.dma_start(out=out[index * P : (index + 1) * P, cols], in_=image[:])
 
         steps = SLICES * GROUPS * PACK
+        tiles = V // P
+        sorted_words = {}
         logs = {}
         ods = {}
         hbs = {}
         invs = {}
         next_image = 0
+        next_inv = 0
+        last_hb = FIRST_TURN + PERIOD * (GROUPS - 1) + HB_LAG + PACK + 1
+        sort_channels(0)
+        later_loads()
         for step in range(steps):
             s, rest = divmod(step, GROUPS * PACK)
             g, block = divmod(rest, PACK)
-            if step in TURN_AT:
-                logs[TURN_AT.index(step)] = turn_and_log(TURN_AT.index(step))
-            if step == 0:
-                sort_channels(0)
+            helping = step < FIRST_TURN
             if step == 2:
                 sort_channels(1)
-            if step == WEIGH_AT[0]:
-                nc.vector.tensor_copy(
-                    out=weight_run[:], in_=weight_raw[:].unsqueeze(1).to_broadcast([P, 8, PACK])
-                )
             if step == 5:
                 sort_channels(2)
             if step == 7:
                 pack_unmix()
-            if step == HB_AT[0]:
-                spread_coupling()
-            if step in WEIGH_AT:
-                ods[WEIGH_AT.index(step)] = weigh(logs[WEIGH_AT.index(step)])
             if step == 9:
                 quantize(unmix_codes, unmix_plane, unmix_packed)
-            if step - 3 in WEIGH_AT:
-                gg = WEIGH_AT.index(step - 3)
-                quantize(od_codes[gg], od_plane[gg], ods[gg])
             for gg in range(GROUPS):
-                if 0 <= step - HB_AT[gg] < PACK:
-                    if step == HB_AT[gg]:
-                        hbs[gg] = stage.tile([P, C, PACK], BF16, name="hb", align_bytes=ALIGN)
-                    hb_block(gg, hbs[gg], step - HB_AT[gg])
-                if step - HB_AT[gg] == PACK + 1:
+                lag = step - FIRST_TURN - PERIOD * gg
+                if PRESORT and lag == (-1 if gg == 0 else -2):
+                    sorted_words[gg] = sort_words(gg)
+                if lag == 0:
+                    logs[gg] = turn_and_log(gg, sorted_words.get(gg))
+                if 0 <= lag < (2 if gg == 0 else HELP):
+                    helping = True
+                if lag == WEIGH_LAG:
+                    if gg == 0:
+                        nc.vector.tensor_copy(
+                            out=weight_run[:], in_=weight_raw[:].unsqueeze(1).to_broadcast([P, 8, PACK])
+                        )
+                    ods[gg] = weigh(logs[gg])
+                if lag == OD_LAG:
+                    quantize(od_codes[gg], od_plane[gg], ods[gg])
+                if lag == HB_LAG:
+                    hbs[gg] = stage.tile([P, C, PACK], BF16, name="hb", align_bytes=ALIGN)
+                if HB_LAG <= lag < HB_LAG + PACK:
+                    hb_block(gg, hbs[gg], lag - HB_LAG)
+                if lag == HB_LAG + PACK + 1:
                     quantize(hb_codes[gg], hb_plane[gg], hbs[gg])
             if block == 0:
-                invs[(s, g)] = stream.tile([P, K_PASS, PACK], BF16, name="inv", align_bytes=ALIGN)
-            inv_block(s, g, invs[(s, g)], block, step >= WIDE_FROM, step in VECTOR_STEPS)
-            if block == 1 and step > PACK:
-                done = divmod(step // PACK - 1, GROUPS)
+                invs[(s, g)] = keep.tile([P, K_PASS, PACK], BF16, name="inv%d_%d" % (s, g), align_bytes=ALIGN)
+            inv_block(s, g, invs[(s, g)], block, step >= WIDE_FROM, helping)
+            lag_now = INV_LAG if step < last_hb - 4 else 2
+            if step + 1 - lag_now >= PACK * (next_inv + 1):
+                done = divmod(next_inv, GROUPS)
                 quantize(inv_codes[done], inv_plane[done], invs[done])
-            if step > OUT_FROM and next_image < V // P - HELD_BACK:
-                image_tile(next_image, True)
+                next_inv = next_inv + 1
+            if step > last_hb and next_image < tiles - PACK - HELD_BACK and next_image // PACK < next_inv // GROUPS and (step - last_hb) % IMG_EVERY == 0:
+                image_tile(next_image, slice(0, C), True)
                 next_image = next_image + 1
-        last = (SLICES - 1, GROUPS - 1)
-        quantize(inv_codes[last], inv_plane[last], invs[last])
-        for index in range(next_image, V // P):
-            image_tile(index, index % 2 == 1)
+        for n in range(next_inv, SLICES * GROUPS):
+            done = divmod(n, GROUPS)
+            quantize(inv_codes[done], inv_plane[done], invs[done])
+        for index in range(next_image, tiles - 1):
+            image_tile(index, slice(0, C), index % 2 == 1)
+        for half in range(2):
+            image_tile(tiles - 1, slice(half * C // 2, (half + 1) * C // 2), half == 0)

@@ -3,8 +3,8 @@ from contextlib import ExitStack
 import concourse.mybir as mybir
 from concourse.masks import make_identity
 
-V, D, MODES, L, C = 2048, 1536, 1024, 512, 512
-FLOPS = 2 * V * D * MODES + 2 * D * L * C + 2 * V * D * C
+VOXELS, CHANNELS, MODES, WAVELENGTHS, COLUMNS = 2048, 1536, 1024, 512, 512
+FLOPS = 2 * VOXELS * CHANNELS * MODES + 2 * CHANNELS * WAVELENGTHS * COLUMNS + 2 * VOXELS * CHANNELS * COLUMNS
 
 F32 = mybir.dt.float32
 BF16 = mybir.dt.bfloat16
@@ -17,24 +17,23 @@ ACT = mybir.ActivationFunctionType
 ALU = mybir.AluOpType
 
 P = 128
-PACK = 4
-K_PASS = P * PACK
+SLOTS = 4
+K_PASS = P * SLOTS
+BANK = 512
+RUN = 8
+QUADRANTS = 4
 MODE_PASSES = MODES // K_PASS
-GROUPS = D // K_PASS
-SLICES = V // K_PASS
+GROUPS = CHANNELS // K_PASS
+SLICE = 512
+SLICES = VOXELS // SLICE
+BANKS_PER_PART = SLICE * SLOTS // BANK
 ALIGN = 64
 
-FIRST_TURN = 2
-PERIOD = 9
-WEIGH_LAG = 3
-OD_LAG = 6
-HB_LAG = 12
-HELP = 0
-WIDE_FROM = 28
-HELD_BACK = 2
-PRESORT = False
-INV_LAG = 2
-IMG_EVERY = 1
+STEPS = SLICES * GROUPS * BANKS_PER_PART
+GAP = 3
+PERIOD = 10
+HB_LAG = 14
+WIDE_FROM = 32
 
 
 def tile_optical_tomography_unmixing_s12_kernel(
@@ -43,163 +42,171 @@ def tile_optical_tomography_unmixing_s12_kernel(
     nc = tc.nc
     with ExitStack() as ctx:
         keep = ctx.enter_context(tc.tile_pool(name="keep", bufs=1))
-        stage = ctx.enter_context(tc.tile_pool(name="stage", bufs=2))
-        stream = ctx.enter_context(tc.tile_pool(name="stream", bufs=4))
+        chain = ctx.enter_context(tc.tile_pool(name="chain", bufs=2))
+        stores = ctx.enter_context(tc.tile_pool(name="stores", bufs=8))
         psum = ctx.enter_context(tc.psum_pool(name="psum", bufs=8))
         ctx.enter_context(tc.manual_schedule())
 
         def kept(name, shape, dtype):
             return keep.tile(shape, dtype, name=name, align_bytes=ALIGN)
 
-        def new_bank(dtype):
-            width = K_PASS if dtype == F32 else 2 * K_PASS
-            return psum.tile([P, width], dtype, name="bank", tag="bank")
+        def new_bank():
+            return psum.tile([P, BANK], F32, name="bank")
 
-        vox_codes = [kept("vox_codes%d" % s, [P, MODE_PASSES, 2 * K_PASS], U8) for s in range(SLICES)]
-        vox_plane_first = kept("vox_plane_first", [P, MODE_PASSES, K_PASS], U8)
-        vox_plane_rest = kept("vox_plane_rest", [P, MODE_PASSES, V - K_PASS], U8)
+        parts = [(s, g) for s in range(SLICES) for g in range(GROUPS)]
+
+        vox_codes = [kept("vox_codes%d" % s, [P, MODE_PASSES, 2 * SLICE], U8) for s in range(SLICES)]
+        vox_plane_first = kept("vox_plane_first", [P, MODE_PASSES, SLICE], U8)
+        vox_plane_rest = kept("vox_plane_rest", [P, MODE_PASSES, VOXELS - SLICE], U8)
         chan_raw = [kept("chan_raw%d" % g, [P, MODE_PASSES, 2 * K_PASS], U8) for g in range(GROUPS)]
-        chan_plane_first = kept("chan_plane_first", [P, MODE_PASSES, K_PASS], U8)
-        chan_plane_rest = kept("chan_plane_rest", [P, MODE_PASSES, D - K_PASS], U8)
-        chan_codes = [kept("chan_codes%d" % g, [P, MODE_PASSES, PACK, 2 * P], U8) for g in range(GROUPS)]
-        chan_plane = [kept("chan_plane%d" % g, [P, MODE_PASSES, PACK, P], U8) for g in range(GROUPS)]
-        ratio_rows = [kept("ratio_rows%d" % g, [P, PACK, L], BF16) for g in range(GROUPS)]
-        unmix_raw = kept("unmix_raw", [P, PACK, C], BF16)
-        unmix_packed = kept("unmix_packed", [P, C, PACK], BF16)
-        unmix_codes = kept("unmix_codes", [P, C], U32)
-        unmix_plane = kept("unmix_plane", [P, C], U8)
-        weight_raw = kept("weight_raw", [P, PACK], BF16)
-        weight_run = kept("weight_run", [P, 8, PACK], F32)
+        chan_raw_plane_first = kept("chan_raw_plane_first", [P, MODE_PASSES, K_PASS], U8)
+        chan_raw_plane_rest = kept("chan_raw_plane_rest", [P, MODE_PASSES, CHANNELS - K_PASS], U8)
+        chan_codes = [kept("chan_codes%d" % g, [P, MODE_PASSES, SLOTS, 2 * P], U8) for g in range(GROUPS)]
+        chan_plane = [kept("chan_plane%d" % g, [P, MODE_PASSES, SLOTS, P], U8) for g in range(GROUPS)]
+        ratio_rows = [kept("ratio_rows%d" % g, [P, SLOTS, WAVELENGTHS], BF16) for g in range(GROUPS)]
+        unmix_raw = kept("unmix_raw", [P, SLOTS, COLUMNS], BF16)
+        unmix_packed = kept("unmix_packed", [P, COLUMNS, SLOTS], BF16)
+        unmix_codes = kept("unmix_codes", [P, COLUMNS], U32)
+        unmix_plane = kept("unmix_plane", [P, COLUMNS], U8)
+        weight_raw = kept("weight_raw", [P, SLOTS], BF16)
+        weight_run = kept("weight_run", [P, RUN, SLOTS], F32)
         coupling_rows = kept("coupling_rows", [P, GROUPS * P], BF16)
-        coupling_slots = kept("coupling_slots", [P, GROUPS, PACK], F32)
+        coupling_slots = kept("coupling_slots", [P, GROUPS, SLOTS], F32)
         ident_f32 = kept("ident_f32", [P, P], F32)
         ident_bf16 = kept("ident_bf16", [P, P], BF16)
         od_codes = [kept("od_codes%d" % g, [P, K_PASS], U32) for g in range(GROUPS)]
         od_plane = [kept("od_plane%d" % g, [P, K_PASS], U8) for g in range(GROUPS)]
-        hb_codes = [kept("hb_codes%d" % g, [P, C], U32) for g in range(GROUPS)]
-        hb_plane = [kept("hb_plane%d" % g, [P, C], U8) for g in range(GROUPS)]
-        inv_codes = {}
-        inv_plane = {}
-        for s in range(SLICES):
-            for g in range(GROUPS):
-                inv_codes[(s, g)] = kept("inv_codes%d_%d" % (s, g), [P, K_PASS], U32)
-                inv_plane[(s, g)] = kept("inv_plane%d_%d" % (s, g), [P, K_PASS], U8)
-
-        nc.gpsimd.memset(chan_plane_first[:].bitcast(I32), 0)
-        nc.gpsimd.memset(vox_plane_first[:].bitcast(I32), 0)
-
-        def load_codes(dst, words, index):
-            cols = slice(index * 256, (index + 1) * 256)
-            nc.sync.dma_start(out=dst[:].bitcast(I32), in_=words.bitcast(I32)[:, :, cols].rearrange("g p w -> p g w"))
-
-        def load_plane(dst, scales, cols, queues):
-            for quad, queue in enumerate(queues):
-                queue.dma_start(
-                    out=dst[32 * quad : 32 * quad + 4, :, :].bitcast(I32),
-                    in_=scales.bitcast(I32)[:, 4 * quad : 4 * quad + 4, cols].rearrange("g r w -> r g w"),
-                )
-
-        def load_ratio(g):
-            rows = ratio[g * K_PASS : (g + 1) * K_PASS, :]
-            nc.sync.dma_start(out=ratio_rows[g][:], in_=rows.rearrange("(m j) l -> m j l", j=PACK))
-
-        first = slice(0, P)
-        on_sync = (nc.sync, nc.sync, nc.sync, nc.sync)
-        load_codes(chan_raw[0], chan_words, 0)
-        load_codes(vox_codes[0], vox_words, 0)
-        load_plane(chan_plane_first, chan_scales, first, on_sync)
-        load_plane(vox_plane_first, vox_scales, first, (nc.gpsimd, nc.gpsimd, nc.sync, nc.sync))
-        make_identity(nc, ident_f32[:])
-        nc.gpsimd.memset(coupling_rows[:], 0.0)
-        make_identity(nc, ident_bf16[:])
-        load_ratio(0)
-        load_codes(chan_raw[1], chan_words, 1)
-
-        def later_loads():
-            nc.vector.memset(chan_plane_rest[:].bitcast(I32), 0)
-            nc.vector.memset(vox_plane_rest[:].bitcast(I32), 0)
-            load_plane(chan_plane_rest, chan_scales, slice(P, D // 4), on_sync)
-            nc.sync.dma_start(out=weight_raw[:], in_=bin_weight.rearrange("(p t) -> p t", t=PACK))
-            load_codes(chan_raw[2], chan_words, 2)
-            nc.sync.dma_start(out=unmix_raw[:], in_=unmix.rearrange("(p j) c -> p j c", j=PACK))
-            load_plane(vox_plane_rest, vox_scales, slice(P, V // 4), on_sync)
-            load_codes(vox_codes[1], vox_words, 1)
-            nc.sync.dma_start(
-                out=coupling_rows[0:PACK, :].rearrange("t (b r) -> t b r", r=8),
-                in_=coupling.rearrange("(b t r) -> t b r", t=PACK, r=8),
-            )
-            load_ratio(1)
-            load_codes(vox_codes[2], vox_words, 2)
-            load_ratio(2)
-            load_codes(vox_codes[3], vox_words, 3)
-
-        def group_of(first_tile, rest_tile, index):
-            if index == 0:
-                return first_tile[:]
-            return rest_tile[:, :, (index - 1) * K_PASS : index * K_PASS]
+        hb_codes = [kept("hb_codes%d" % g, [P, COLUMNS], U32) for g in range(GROUPS)]
+        hb_plane = [kept("hb_plane%d" % g, [P, COLUMNS], U8) for g in range(GROUPS)]
+        inv_packed = {part: kept("inv_packed%d_%d" % part, [P, SLICE, SLOTS], BF16) for part in parts}
+        inv_codes = {part: kept("inv_codes%d_%d" % part, [P, SLICE], U32) for part in parts}
+        inv_plane = {part: kept("inv_plane%d_%d" % part, [P, SLICE], U8) for part in parts}
 
         def quantize(codes, plane, packed):
             nc.vector.quantize_mx(
                 out=codes[:].bitcast(FP8X4), scales=plane[:], in_=packed[:].rearrange("p c t -> p (c t)")
             )
 
-        def sort_channels(g):
+        make_identity(nc, ident_f32[:])
+        nc.vector.memset(vox_plane_first[:].bitcast(I32), 0)
+        for plane in (chan_plane[0], chan_raw_plane_rest, vox_plane_rest):
+            nc.vector.memset(plane[:].bitcast(I32), 0)
+        nc.gpsimd.memset(coupling_rows[:], 0.0)
+        make_identity(nc, ident_bf16[:])
+
+        def load_codes(dst, words, index):
+            width = dst.shape[2] // 4
+            src = words.bitcast(I32)[:, :, index * width : (index + 1) * width]
+            nc.sync.dma_start(out=dst[:].bitcast(I32), in_=src.rearrange("k p w -> p k w"))
+
+        def load_plane(dst, scales, first_column):
+            cols = slice(first_column // 4, (first_column + dst.shape[2]) // 4)
+            for quad in range(QUADRANTS):
+                nc.sync.dma_start(
+                    out=dst[32 * quad : 32 * quad + 4].bitcast(I32),
+                    in_=scales.bitcast(I32)[:, 4 * quad : 4 * quad + 4, cols].rearrange("k r w -> r k w"),
+                )
+
+        def load_ratio(g):
+            rows = ratio[g * K_PASS : (g + 1) * K_PASS, :]
+            nc.sync.dma_start(
+                out=ratio_rows[g][:].rearrange("m (a j) l -> m a j l", j=2),
+                in_=rows.rearrange("(a m j) l -> m a j l", a=2, j=2),
+            )
+
+        load_plane(chan_raw_plane_first, chan_scales, 0)
+        load_ratio(0)
+        load_codes(chan_raw[0], chan_words, 0)
+        load_codes(vox_codes[0], vox_words, 0)
+        load_plane(vox_plane_first, vox_scales, 0)
+        load_codes(chan_raw[1], chan_words, 1)
+        load_plane(chan_raw_plane_rest, chan_scales, K_PASS)
+        nc.sync.dma_start(out=weight_raw[:], in_=bin_weight.rearrange("(p t) -> p t", t=SLOTS))
+        load_codes(chan_raw[2], chan_words, 2)
+        nc.sync.dma_start(out=unmix_raw[:], in_=unmix.rearrange("(p t) c -> p t c", t=SLOTS))
+        load_ratio(1)
+        load_plane(vox_plane_rest, vox_scales, SLICE)
+        nc.sync.dma_start(
+            out=coupling_rows[0:SLOTS, :].rearrange("t (b r) -> t b r", r=RUN),
+            in_=coupling.rearrange("(b t r) -> t b r", t=SLOTS, r=RUN),
+        )
+        load_codes(vox_codes[1], vox_words, 1)
+        load_codes(vox_codes[2], vox_words, 2)
+        load_ratio(2)
+        load_codes(vox_codes[3], vox_words, 3)
+
+        def plane_part(first_tile, rest_tile, index):
+            width = first_tile.shape[2]
+            if index == 0:
+                return first_tile[:]
+            return rest_tile[:, :, (index - 1) * width : index * width]
+
+        def sort_codes(g):
             nc.vector.tensor_copy(
                 out=chan_codes[g][:].bitcast(I32).rearrange("p k t (q w) -> p k t q w", w=4),
-                in_=chan_raw[g][:].bitcast(I32).rearrange("p k (q t w) -> p k t q w", t=PACK, w=4),
-            )
-            nc.vector.tensor_copy(
-                out=chan_plane[g][:].bitcast(I32).rearrange("p k t (q w) -> p k t q w", w=2),
-                in_=group_of(chan_plane_first, chan_plane_rest, g).bitcast(I32).rearrange(
-                    "p k (q t w) -> p k t q w", t=PACK, w=2
-                ),
+                in_=chan_raw[g][:].bitcast(I32).rearrange("p k (q t w) -> p k t q w", t=SLOTS, w=4),
             )
 
-        def sort_words(g):
-            words = stage.tile([P, PACK, 2, P], F32, name="words")
+        def sort_plane(g, rows):
+            raw = plane_part(chan_raw_plane_first, chan_raw_plane_rest, g)
             nc.vector.tensor_copy(
-                out=words[:], in_=ratio_rows[g][:].bitcast(F32).rearrange("p j (w u) -> p j u w", u=2)
+                out=chan_plane[g][rows].bitcast(I32).rearrange("p k t (q w) -> p k t q w", w=2),
+                in_=raw[rows].bitcast(I32).rearrange("p k (q t w) -> p k t q w", t=SLOTS, w=2),
             )
-            return words
 
-        def turn_and_log(g, words):
-            log_ratio = stage.tile([P, P, PACK, PACK], F32, name="log_ratio")
+        def pairs_in_place(g):
+            return ratio_rows[g][:].bitcast(F32).rearrange("m j (p u) -> m j u p", u=2)
+
+        def sort_pairs(g):
+            pairs = chain.tile([P, SLOTS, 2, P], F32, name="pairs")
+            nc.vector.tensor_copy(out=pairs[:], in_=pairs_in_place(g))
+            return pairs
+
+        def transpose_pairs(pairs):
             banks = []
-            for half in range(2):
-                bank = new_bank(F32)
-                for jj in range(2):
+            for a in range(2):
+                bank = new_bank()
+                for j in range(2):
                     for u in range(2):
-                        quarter = 2 * jj + u
-                        src = words[:, 2 * half + jj, u, :] if PRESORT else ratio_rows[g][:].bitcast(F32)[:, 2 * half + jj, u::2]
-                        nc.tensor.transpose(bank[:, quarter * P : (quarter + 1) * P], src, ident_f32[:])
+                        quarter = 2 * j + u
+                        nc.tensor.transpose(
+                            bank[:, quarter * P : (quarter + 1) * P], pairs[:, 2 * a + j, u, :], ident_f32[:]
+                        )
                 banks.append(bank)
-            if g == 1:
-                spread_coupling()
-            for half in range(2):
+            return banks
+
+        def take_logs(banks):
+            log_ratio = chain.tile([P, K_PASS, SLOTS], F32, name="log_ratio")
+            for a, bank in enumerate(banks):
+                dst = log_ratio[:, a * 2 * P : (a + 1) * 2 * P, :]
                 nc.scalar.activation(
-                    out=log_ratio[:, :, 2 * half : 2 * half + 2, :].rearrange("p m j (u e) -> p m (j u) e", e=2),
-                    in_=banks[half][:].bitcast(BF16).rearrange("p (a m e) -> p m a e", a=PACK, e=2),
+                    out=dst.rearrange("p (m j) (u e) -> p m (j u) e", j=2, e=2),
+                    in_=bank[:].bitcast(BF16).rearrange("p (quarter m e) -> p m quarter e", m=P, e=2),
                     func=ACT.Ln,
                 )
             return log_ratio
 
         def weigh(log_ratio):
-            od = stage.tile([P, K_PASS, PACK], BF16, name="od", align_bytes=ALIGN)
+            od = chain.tile([P, K_PASS, SLOTS], BF16, name="od", align_bytes=ALIGN)
+            weights = weight_run[:].rearrange("p r s -> p (r s)").unsqueeze(1).unsqueeze(1)
             nc.vector.tensor_tensor(
-                out=od[:].rearrange("p (t q r) s -> p t q (r s)", t=PACK, r=8),
-                in0=log_ratio[:].rearrange("p (q t h) j s -> p t q (h j s)", t=PACK, h=2),
-                in1=weight_run[:].rearrange("p r s -> p (r s)").unsqueeze(1).unsqueeze(1).to_broadcast([P, PACK, 16, 32]),
+                out=od[:].rearrange("p (t q r) s -> p t q (r s)", t=SLOTS, r=RUN),
+                in0=log_ratio[:].rearrange("p (q t r) s -> p t q (r s)", t=SLOTS, r=RUN),
+                in1=weights.to_broadcast([P, SLOTS, P // RUN, RUN * SLOTS]),
                 op=ALU.mult,
             )
             return od
 
+        def spread_weight():
+            nc.vector.tensor_copy(out=weight_run[:], in_=weight_raw[:].unsqueeze(1).to_broadcast([P, RUN, SLOTS]))
+
         def spread_coupling():
-            bank = new_bank(BF16)
+            turned = psum.tile([P, 2 * BANK], BF16, name="bank")
             for g in range(GROUPS):
-                nc.tensor.transpose(bank[:, g * P : (g + 1) * P], coupling_rows[:, g * P : (g + 1) * P], ident_bf16[:])
-            nc.vector.tensor_copy(
-                out=coupling_slots[:], in_=bank[:, 0 : GROUPS * P].rearrange("p (g x) -> p g x", x=P)[:, :, 0:PACK]
-            )
+                cols = slice(g * P, (g + 1) * P)
+                nc.tensor.transpose(turned[:, cols], coupling_rows[:, cols], ident_bf16[:])
+            by_group = turned[:, 0 : GROUPS * P].rearrange("p (g row) -> p g row", row=P)
+            nc.vector.tensor_copy(out=coupling_slots[:], in_=by_group[:, :, 0:SLOTS])
 
         def pack_unmix():
             nc.vector.tensor_copy(
@@ -207,10 +214,10 @@ def tile_optical_tomography_unmixing_s12_kernel(
                 in_=unmix_raw[:].rearrange("p t (c i) -> p c t i", i=4),
             )
 
-        def hb_block(g, hb, block):
+        def hb_bank(g, hb, block):
             cols = slice(block * P, (block + 1) * P)
-            bank = new_bank(F32)
-            for t in range(PACK):
+            bank = new_bank()
+            for t in range(SLOTS):
                 slot = slice(t * P, (t + 1) * P)
                 nc.tensor.matmul_mx(
                     out=bank[:, slot],
@@ -223,40 +230,46 @@ def tile_optical_tomography_unmixing_s12_kernel(
                 )
             nc.vector.tensor_tensor(
                 out=hb[:, cols, :],
-                in0=bank[:].rearrange("p (t c) -> p c t", t=PACK),
-                in1=coupling_slots[:, g, :].unsqueeze(1).to_broadcast([P, P, PACK]),
+                in0=bank[:].rearrange("p (t c) -> p c t", t=SLOTS),
+                in1=coupling_slots[:, g, :].unsqueeze(1).to_broadcast([P, P, SLOTS]),
                 op=ALU.mult,
             )
 
-        def inv_block(s, g, inv, block, wide, on_vector):
-            bank = new_bank(F32)
-            width = 2 * P if wide else P
-            start = (block // 2) * width if wide else block * width
-            slots = range(2 * (block % 2), 2 * (block % 2) + 2) if wide else range(PACK)
-            plane = group_of(vox_plane_first, vox_plane_rest, s)
+        def inv_bank(step):
+            part_index, piece = divmod(step, BANKS_PER_PART)
+            s, g = parts[part_index]
+            if step < WIDE_FROM:
+                width, first_voxel, slots = P, piece * P, range(SLOTS)
+            else:
+                width, first_voxel, slots = 2 * P, (piece % 2) * 2 * P, range(piece - piece % 2, piece - piece % 2 + 2)
+            voxels = slice(first_voxel, first_voxel + width)
+            plane = plane_part(vox_plane_first, vox_plane_rest, s)
+            bank = new_bank()
             for i, t in enumerate(slots):
                 for k in range(MODE_PASSES):
                     nc.tensor.matmul_mx(
                         out=bank[:, i * width : (i + 1) * width],
                         lhsT=chan_codes[g][:, k, t, :].bitcast(FP4X4),
                         lhsT_scale=chan_plane[g][:, k, t, :],
-                        rhs=vox_codes[s][:, k, 2 * start : 2 * (start + width)].bitcast(FP4X4),
-                        rhs_scale=plane[:, k, start : start + width],
+                        rhs=vox_codes[s][:, k, 2 * voxels.start : 2 * voxels.stop].bitcast(FP4X4),
+                        rhs_scale=plane[:, k, voxels],
                         start=(k == 0),
                         stop=(k == MODE_PASSES - 1),
                     )
-            dst = inv[:, start : start + width, slots.start : slots.stop]
-            src = bank[:].rearrange("p (t v) -> p v t", v=width)
-            if on_vector:
-                nc.vector.tensor_copy(out=dst, in_=src)
-            else:
-                nc.scalar.copy(out=dst, in_=src)
+            nc.scalar.copy(
+                out=inv_packed[(s, g)][:, voxels, slots.start : slots.stop],
+                in_=bank[:].rearrange("p (t v) -> p v t", v=width),
+            )
 
-        def image_tile(index, cols, on_vector):
-            s, block = divmod(index, PACK)
+        def quantize_inv(part_index):
+            part = parts[part_index]
+            quantize(inv_codes[part], inv_plane[part], inv_packed[part])
+
+        def image_tile(index, cols, copy_out):
+            s, block = divmod(index, SLICE // P)
             voxels = slice(block * P, (block + 1) * P)
             width = cols.stop - cols.start
-            bank = new_bank(F32)
+            bank = new_bank()
             for g in range(GROUPS):
                 nc.tensor.matmul_mx(
                     out=bank[:, 0:width],
@@ -267,74 +280,59 @@ def tile_optical_tomography_unmixing_s12_kernel(
                     start=(g == 0),
                     stop=(g == GROUPS - 1),
                 )
-            image = stream.tile([P, width], F32, name="image")
-            if on_vector:
-                nc.vector.tensor_copy(out=image[:], in_=bank[:, 0:width])
-            else:
-                nc.scalar.copy(out=image[:], in_=bank[:, 0:width])
+            image = stores.tile([P, width], F32, name="image")
+            copy_out(out=image[:], in_=bank[:, 0:width])
             nc.sync.dma_start(out=out[index * P : (index + 1) * P, cols], in_=image[:])
 
-        steps = SLICES * GROUPS * PACK
-        tiles = V // P
-        sorted_words = {}
-        logs = {}
-        ods = {}
-        hbs = {}
-        invs = {}
-        next_image = 0
-        next_inv = 0
-        last_hb = FIRST_TURN + PERIOD * (GROUPS - 1) + HB_LAG + PACK + 1
-        sort_channels(0)
-        later_loads()
-        for step in range(steps):
-            s, rest = divmod(step, GROUPS * PACK)
-            g, block = divmod(rest, PACK)
-            helping = step < FIRST_TURN
-            if step == 2:
-                sort_channels(1)
-            if step == 5:
-                sort_channels(2)
-            if step == 7:
+        for quad in range(QUADRANTS):
+            sort_plane(0, slice(32 * quad, 32 * quad + 4))
+        sort_codes(0)
+
+        hb_done = HB_LAG + COLUMNS // P + 1
+        first_image_step = (GROUPS - 1) * PERIOD + hb_done + 2
+        tiles = VOXELS // P
+        woven_images = STEPS - first_image_step
+        pairs = {0: pairs_in_place(0)}
+        logs, ods, hbs = {}, {}, {}
+        for step in range(STEPS):
+            if 0 < step < GROUPS:
+                sort_codes(step)
+                sort_plane(step, slice(0, P))
+            if step == GAP:
+                spread_weight()
+            if step == 2 * GAP:
                 pack_unmix()
-            if step == 9:
+            if step == 3 * GAP:
                 quantize(unmix_codes, unmix_plane, unmix_packed)
-            for gg in range(GROUPS):
-                lag = step - FIRST_TURN - PERIOD * gg
-                if PRESORT and lag == (-1 if gg == 0 else -2):
-                    sorted_words[gg] = sort_words(gg)
+            for g in range(GROUPS):
+                lag = step - g * PERIOD
+                if lag == -2 * GAP:
+                    pairs[g] = sort_pairs(g)
                 if lag == 0:
-                    logs[gg] = turn_and_log(gg, sorted_words.get(gg))
-                if 0 <= lag < (2 if gg == 0 else HELP):
-                    helping = True
-                if lag == WEIGH_LAG:
-                    if gg == 0:
-                        nc.vector.tensor_copy(
-                            out=weight_run[:], in_=weight_raw[:].unsqueeze(1).to_broadcast([P, 8, PACK])
-                        )
-                    ods[gg] = weigh(logs[gg])
-                if lag == OD_LAG:
-                    quantize(od_codes[gg], od_plane[gg], ods[gg])
+                    banks = transpose_pairs(pairs[g])
+                    if g == 1:
+                        spread_coupling()
+                    logs[g] = take_logs(banks)
+                if lag == GAP:
+                    ods[g] = weigh(logs[g])
+                if lag == 2 * GAP:
+                    quantize(od_codes[g], od_plane[g], ods[g])
                 if lag == HB_LAG:
-                    hbs[gg] = stage.tile([P, C, PACK], BF16, name="hb", align_bytes=ALIGN)
-                if HB_LAG <= lag < HB_LAG + PACK:
-                    hb_block(gg, hbs[gg], lag - HB_LAG)
-                if lag == HB_LAG + PACK + 1:
-                    quantize(hb_codes[gg], hb_plane[gg], hbs[gg])
-            if block == 0:
-                invs[(s, g)] = keep.tile([P, K_PASS, PACK], BF16, name="inv%d_%d" % (s, g), align_bytes=ALIGN)
-            inv_block(s, g, invs[(s, g)], block, step >= WIDE_FROM, helping)
-            lag_now = INV_LAG if step < last_hb - 4 else 2
-            if step + 1 - lag_now >= PACK * (next_inv + 1):
-                done = divmod(next_inv, GROUPS)
-                quantize(inv_codes[done], inv_plane[done], invs[done])
-                next_inv = next_inv + 1
-            if step > last_hb and next_image < tiles - PACK - HELD_BACK and next_image // PACK < next_inv // GROUPS and (step - last_hb) % IMG_EVERY == 0:
-                image_tile(next_image, slice(0, C), True)
-                next_image = next_image + 1
-        for n in range(next_inv, SLICES * GROUPS):
-            done = divmod(n, GROUPS)
-            quantize(inv_codes[done], inv_plane[done], invs[done])
-        for index in range(next_image, tiles - 1):
-            image_tile(index, slice(0, C), index % 2 == 1)
+                    hbs[g] = chain.tile([P, COLUMNS, SLOTS], BF16, name="hb", align_bytes=ALIGN)
+                if HB_LAG <= lag < HB_LAG + COLUMNS // P:
+                    hb_bank(g, hbs[g], lag - HB_LAG)
+                if lag == hb_done:
+                    quantize(hb_codes[g], hb_plane[g], hbs[g])
+            inv_bank(step)
+            finished, since = divmod(step + 1 - GAP, BANKS_PER_PART)
+            if since == 0 and finished > 0:
+                quantize_inv(finished - 1)
+            if 0 <= step - first_image_step < woven_images:
+                image_tile(step - first_image_step, slice(0, COLUMNS), nc.vector.tensor_copy)
+
+        quantize_inv(len(parts) - 1)
+        copies = (nc.scalar.copy, nc.vector.tensor_copy)
+        for index in range(woven_images, tiles - 1):
+            image_tile(index, slice(0, COLUMNS), copies[index % 2])
         for half in range(2):
-            image_tile(tiles - 1, slice(half * C // 2, (half + 1) * C // 2), half == 0)
+            image_tile(tiles - 1, slice(half * COLUMNS // 2, (half + 1) * COLUMNS // 2), copies[1 - half])

from contextlib import ExitStack

import concourse.mybir as mybir
from concourse.masks import make_identity

VOXELS, CHANNELS, MODES, WAVELENGTHS, COLUMNS = 2048, 1536, 1024, 512, 512
FLOPS = 2 * VOXELS * CHANNELS * MODES + 2 * CHANNELS * WAVELENGTHS * COLUMNS + 2 * VOXELS * CHANNELS * COLUMNS

F32 = mybir.dt.float32
BF16 = mybir.dt.bfloat16
I32 = mybir.dt.int32
U32 = mybir.dt.uint32
U8 = mybir.dt.uint8
FP8X4 = mybir.dt.float8_e4m3fn_x4
FP4X4 = mybir.dt.float4_e2m1fn_x4
ACT = mybir.ActivationFunctionType
ALU = mybir.AluOpType

P = 128
SLOTS = 4
K_PASS = P * SLOTS
BANK = 512
RUN = 8
QUADRANTS = 4
MODE_PASSES = MODES // K_PASS
GROUPS = CHANNELS // K_PASS
SLICE = 512
SLICES = VOXELS // SLICE
BANKS_PER_PART = SLICE * SLOTS // BANK
ALIGN = 64

STEPS = SLICES * GROUPS * BANKS_PER_PART
GAP = 3
PERIOD = 10
HB_LAG = 14
WIDE_FROM = 32


def tile_optical_tomography_unmixing_s12_kernel(
    tc, vox_words, vox_scales, chan_words, chan_scales, ratio, bin_weight, unmix, coupling, out
):
    nc = tc.nc
    with ExitStack() as ctx:
        keep = ctx.enter_context(tc.tile_pool(name="keep", bufs=1))
        chain = ctx.enter_context(tc.tile_pool(name="chain", bufs=2))
        stores = ctx.enter_context(tc.tile_pool(name="stores", bufs=8))
        psum = ctx.enter_context(tc.psum_pool(name="psum", bufs=8))
        ctx.enter_context(tc.manual_schedule())

        def kept(name, shape, dtype):
            return keep.tile(shape, dtype, name=name, align_bytes=ALIGN)

        def new_bank():
            return psum.tile([P, BANK], F32, name="bank")

        parts = [(s, g) for s in range(SLICES) for g in range(GROUPS)]

        vox_codes = [kept("vox_codes%d" % s, [P, MODE_PASSES, 2 * SLICE], U8) for s in range(SLICES)]
        vox_plane_first = kept("vox_plane_first", [P, MODE_PASSES, SLICE], U8)
        vox_plane_rest = kept("vox_plane_rest", [P, MODE_PASSES, VOXELS - SLICE], U8)
        chan_raw = [kept("chan_raw%d" % g, [P, MODE_PASSES, 2 * K_PASS], U8) for g in range(GROUPS)]
        chan_raw_plane_first = kept("chan_raw_plane_first", [P, MODE_PASSES, K_PASS], U8)
        chan_raw_plane_rest = kept("chan_raw_plane_rest", [P, MODE_PASSES, CHANNELS - K_PASS], U8)
        chan_codes = [kept("chan_codes%d" % g, [P, MODE_PASSES, SLOTS, 2 * P], U8) for g in range(GROUPS)]
        chan_plane = [kept("chan_plane%d" % g, [P, MODE_PASSES, SLOTS, P], U8) for g in range(GROUPS)]
        ratio_rows = [kept("ratio_rows%d" % g, [P, SLOTS, WAVELENGTHS], BF16) for g in range(GROUPS)]
        unmix_raw = kept("unmix_raw", [P, SLOTS, COLUMNS], BF16)
        unmix_packed = kept("unmix_packed", [P, COLUMNS, SLOTS], BF16)
        unmix_codes = kept("unmix_codes", [P, COLUMNS], U32)
        unmix_plane = kept("unmix_plane", [P, COLUMNS], U8)
        weight_raw = kept("weight_raw", [P, SLOTS], BF16)
        weight_run = kept("weight_run", [P, RUN, SLOTS], F32)
        coupling_rows = kept("coupling_rows", [P, GROUPS * P], BF16)
        coupling_slots = kept("coupling_slots", [P, GROUPS, SLOTS], F32)
        ident_f32 = kept("ident_f32", [P, P], F32)
        ident_bf16 = kept("ident_bf16", [P, P], BF16)
        od_codes = [kept("od_codes%d" % g, [P, K_PASS], U32) for g in range(GROUPS)]
        od_plane = [kept("od_plane%d" % g, [P, K_PASS], U8) for g in range(GROUPS)]
        hb_codes = [kept("hb_codes%d" % g, [P, COLUMNS], U32) for g in range(GROUPS)]
        hb_plane = [kept("hb_plane%d" % g, [P, COLUMNS], U8) for g in range(GROUPS)]
        inv_packed = {part: kept("inv_packed%d_%d" % part, [P, SLICE, SLOTS], BF16) for part in parts}
        inv_codes = {part: kept("inv_codes%d_%d" % part, [P, SLICE], U32) for part in parts}
        inv_plane = {part: kept("inv_plane%d_%d" % part, [P, SLICE], U8) for part in parts}

        def quantize(codes, plane, packed):
            nc.vector.quantize_mx(
                out=codes[:].bitcast(FP8X4), scales=plane[:], in_=packed[:].rearrange("p c t -> p (c t)")
            )

        make_identity(nc, ident_f32[:])
        nc.vector.memset(vox_plane_first[:].bitcast(I32), 0)
        for plane in (chan_plane[0], chan_raw_plane_rest, vox_plane_rest):
            nc.vector.memset(plane[:].bitcast(I32), 0)
        nc.gpsimd.memset(coupling_rows[:], 0.0)
        make_identity(nc, ident_bf16[:])

        def load_codes(dst, words, index):
            width = dst.shape[2] // 4
            src = words.bitcast(I32)[:, :, index * width : (index + 1) * width]
            nc.sync.dma_start(out=dst[:].bitcast(I32), in_=src.rearrange("k p w -> p k w"))

        def load_plane(dst, scales, first_column):
            cols = slice(first_column // 4, (first_column + dst.shape[2]) // 4)
            for quad in range(QUADRANTS):
                nc.sync.dma_start(
                    out=dst[32 * quad : 32 * quad + 4].bitcast(I32),
                    in_=scales.bitcast(I32)[:, 4 * quad : 4 * quad + 4, cols].rearrange("k r w -> r k w"),
                )

        def load_ratio(g):
            rows = ratio[g * K_PASS : (g + 1) * K_PASS, :]
            nc.sync.dma_start(
                out=ratio_rows[g][:].rearrange("m (a j) l -> m a j l", j=2),
                in_=rows.rearrange("(a m j) l -> m a j l", a=2, j=2),
            )

        load_plane(chan_raw_plane_first, chan_scales, 0)
        load_ratio(0)
        load_codes(chan_raw[0], chan_words, 0)
        load_codes(vox_codes[0], vox_words, 0)
        load_plane(vox_plane_first, vox_scales, 0)
        load_codes(chan_raw[1], chan_words, 1)
        load_plane(chan_raw_plane_rest, chan_scales, K_PASS)
        nc.sync.dma_start(out=weight_raw[:], in_=bin_weight.rearrange("(p t) -> p t", t=SLOTS))
        load_codes(chan_raw[2], chan_words, 2)
        nc.sync.dma_start(out=unmix_raw[:], in_=unmix.rearrange("(p t) c -> p t c", t=SLOTS))
        load_ratio(1)
        load_plane(vox_plane_rest, vox_scales, SLICE)
        nc.sync.dma_start(
            out=coupling_rows[0:SLOTS, :].rearrange("t (b r) -> t b r", r=RUN),
            in_=coupling.rearrange("(b t r) -> t b r", t=SLOTS, r=RUN),
        )
        load_codes(vox_codes[1], vox_words, 1)
        load_codes(vox_codes[2], vox_words, 2)
        load_ratio(2)
        load_codes(vox_codes[3], vox_words, 3)

        def plane_part(first_tile, rest_tile, index):
            width = first_tile.shape[2]
            if index == 0:
                return first_tile[:]
            return rest_tile[:, :, (index - 1) * width : index * width]

        def sort_codes(g):
            nc.vector.tensor_copy(
                out=chan_codes[g][:].bitcast(I32).rearrange("p k t (q w) -> p k t q w", w=4),
                in_=chan_raw[g][:].bitcast(I32).rearrange("p k (q t w) -> p k t q w", t=SLOTS, w=4),
            )

        def sort_plane(g, rows):
            raw = plane_part(chan_raw_plane_first, chan_raw_plane_rest, g)
            nc.vector.tensor_copy(
                out=chan_plane[g][rows].bitcast(I32).rearrange("p k t (q w) -> p k t q w", w=2),
                in_=raw[rows].bitcast(I32).rearrange("p k (q t w) -> p k t q w", t=SLOTS, w=2),
            )

        def pairs_in_place(g):
            return ratio_rows[g][:].bitcast(F32).rearrange("m j (p u) -> m j u p", u=2)

        def sort_pairs(g):
            pairs = chain.tile([P, SLOTS, 2, P], F32, name="pairs")
            nc.vector.tensor_copy(out=pairs[:], in_=pairs_in_place(g))
            return pairs

        def transpose_pairs(pairs):
            banks = []
            for a in range(2):
                bank = new_bank()
                for j in range(2):
                    for u in range(2):
                        quarter = 2 * j + u
                        nc.tensor.transpose(
                            bank[:, quarter * P : (quarter + 1) * P], pairs[:, 2 * a + j, u, :], ident_f32[:]
                        )
                banks.append(bank)
            return banks

        def take_logs(banks):
            log_ratio = chain.tile([P, K_PASS, SLOTS], F32, name="log_ratio")
            for a, bank in enumerate(banks):
                dst = log_ratio[:, a * 2 * P : (a + 1) * 2 * P, :]
                nc.scalar.activation(
                    out=dst.rearrange("p (m j) (u e) -> p m (j u) e", j=2, e=2),
                    in_=bank[:].bitcast(BF16).rearrange("p (quarter m e) -> p m quarter e", m=P, e=2),
                    func=ACT.Ln,
                )
            return log_ratio

        def weigh(log_ratio):
            od = chain.tile([P, K_PASS, SLOTS], BF16, name="od", align_bytes=ALIGN)
            weights = weight_run[:].rearrange("p r s -> p (r s)").unsqueeze(1).unsqueeze(1)
            nc.vector.tensor_tensor(
                out=od[:].rearrange("p (t q r) s -> p t q (r s)", t=SLOTS, r=RUN),
                in0=log_ratio[:].rearrange("p (q t r) s -> p t q (r s)", t=SLOTS, r=RUN),
                in1=weights.to_broadcast([P, SLOTS, P // RUN, RUN * SLOTS]),
                op=ALU.mult,
            )
            return od

        def spread_weight():
            nc.vector.tensor_copy(out=weight_run[:], in_=weight_raw[:].unsqueeze(1).to_broadcast([P, RUN, SLOTS]))

        def spread_coupling():
            turned = psum.tile([P, 2 * BANK], BF16, name="bank")
            for g in range(GROUPS):
                cols = slice(g * P, (g + 1) * P)
                nc.tensor.transpose(turned[:, cols], coupling_rows[:, cols], ident_bf16[:])
            by_group = turned[:, 0 : GROUPS * P].rearrange("p (g row) -> p g row", row=P)
            nc.vector.tensor_copy(out=coupling_slots[:], in_=by_group[:, :, 0:SLOTS])

        def pack_unmix():
            nc.vector.tensor_copy(
                out=unmix_packed[:].rearrange("p (c i) t -> p c t i", i=4),
                in_=unmix_raw[:].rearrange("p t (c i) -> p c t i", i=4),
            )

        def hb_bank(g, hb, block):
            cols = slice(block * P, (block + 1) * P)
            bank = new_bank()
            for t in range(SLOTS):
                slot = slice(t * P, (t + 1) * P)
                nc.tensor.matmul_mx(
                    out=bank[:, slot],
                    lhsT=od_codes[g][:, slot].bitcast(FP8X4),
                    lhsT_scale=od_plane[g][:, slot],
                    rhs=unmix_codes[:, cols].bitcast(FP8X4),
                    rhs_scale=unmix_plane[:, cols],
                    start=True,
                    stop=True,
                )
            nc.vector.tensor_tensor(
                out=hb[:, cols, :],
                in0=bank[:].rearrange("p (t c) -> p c t", t=SLOTS),
                in1=coupling_slots[:, g, :].unsqueeze(1).to_broadcast([P, P, SLOTS]),
                op=ALU.mult,
            )

        def inv_bank(step):
            part_index, piece = divmod(step, BANKS_PER_PART)
            s, g = parts[part_index]
            if step < WIDE_FROM:
                width, first_voxel, slots = P, piece * P, range(SLOTS)
            else:
                width, first_voxel, slots = 2 * P, (piece % 2) * 2 * P, range(piece - piece % 2, piece - piece % 2 + 2)
            voxels = slice(first_voxel, first_voxel + width)
            plane = plane_part(vox_plane_first, vox_plane_rest, s)
            bank = new_bank()
            for i, t in enumerate(slots):
                for k in range(MODE_PASSES):
                    nc.tensor.matmul_mx(
                        out=bank[:, i * width : (i + 1) * width],
                        lhsT=chan_codes[g][:, k, t, :].bitcast(FP4X4),
                        lhsT_scale=chan_plane[g][:, k, t, :],
                        rhs=vox_codes[s][:, k, 2 * voxels.start : 2 * voxels.stop].bitcast(FP4X4),
                        rhs_scale=plane[:, k, voxels],
                        start=(k == 0),
                        stop=(k == MODE_PASSES - 1),
                    )
            nc.scalar.copy(
                out=inv_packed[(s, g)][:, voxels, slots.start : slots.stop],
                in_=bank[:].rearrange("p (t v) -> p v t", v=width),
            )

        def quantize_inv(part_index):
            part = parts[part_index]
            quantize(inv_codes[part], inv_plane[part], inv_packed[part])

        def image_tile(index, cols, copy_out):
            s, block = divmod(index, SLICE // P)
            voxels = slice(block * P, (block + 1) * P)
            width = cols.stop - cols.start
            bank = new_bank()
            for g in range(GROUPS):
                nc.tensor.matmul_mx(
                    out=bank[:, 0:width],
                    lhsT=inv_codes[(s, g)][:, voxels].bitcast(FP8X4),
                    lhsT_scale=inv_plane[(s, g)][:, voxels],
                    rhs=hb_codes[g][:, cols].bitcast(FP8X4),
                    rhs_scale=hb_plane[g][:, cols],
                    start=(g == 0),
                    stop=(g == GROUPS - 1),
                )
            image = stores.tile([P, width], F32, name="image")
            copy_out(out=image[:], in_=bank[:, 0:width])
            nc.sync.dma_start(out=out[index * P : (index + 1) * P, cols], in_=image[:])

        for quad in range(QUADRANTS):
            sort_plane(0, slice(32 * quad, 32 * quad + 4))
        sort_codes(0)

        hb_done = HB_LAG + COLUMNS // P + 1
        first_image_step = (GROUPS - 1) * PERIOD + hb_done + 2
        tiles = VOXELS // P
        woven_images = STEPS - first_image_step
        pairs = {0: pairs_in_place(0)}
        logs, ods, hbs = {}, {}, {}
        for step in range(STEPS):
            if 0 < step < GROUPS:
                sort_codes(step)
                sort_plane(step, slice(0, P))
            if step == GAP:
                spread_weight()
            if step == 2 * GAP:
                pack_unmix()
            if step == 3 * GAP:
                quantize(unmix_codes, unmix_plane, unmix_packed)
            for g in range(GROUPS):
                lag = step - g * PERIOD
                if lag == -2 * GAP:
                    pairs[g] = sort_pairs(g)
                if lag == 0:
                    banks = transpose_pairs(pairs[g])
                    if g == 1:
                        spread_coupling()
                    logs[g] = take_logs(banks)
                if lag == GAP:
                    ods[g] = weigh(logs[g])
                if lag == 2 * GAP:
                    quantize(od_codes[g], od_plane[g], ods[g])
                if lag == HB_LAG:
                    hbs[g] = chain.tile([P, COLUMNS, SLOTS], BF16, name="hb", align_bytes=ALIGN)
                if HB_LAG <= lag < HB_LAG + COLUMNS // P:
                    hb_bank(g, hbs[g], lag - HB_LAG)
                if lag == hb_done:
                    quantize(hb_codes[g], hb_plane[g], hbs[g])
            inv_bank(step)
            finished, since = divmod(step + 1 - GAP, BANKS_PER_PART)
            if since == 0 and finished > 0:
                quantize_inv(finished - 1)
            if 0 <= step - first_image_step < woven_images:
                image_tile(step - first_image_step, slice(0, COLUMNS), nc.vector.tensor_copy)

        quantize_inv(len(parts) - 1)
        copies = (nc.scalar.copy, nc.vector.tensor_copy)
        for index in range(woven_images, tiles - 1):
            image_tile(index, slice(0, COLUMNS), copies[index % 2])
        for half in range(2):
            image_tile(tiles - 1, slice(half * COLUMNS // 2, (half + 1) * COLUMNS // 2), copies[1 - half])
